import numpy as np
import ml_dtypes


def mxq(x, axis, fmt="e4m3"):
    dtype, down = {"e4m3": (ml_dtypes.float8_e4m3fn, 7), "e5m2": (ml_dtypes.float8_e5m2, 14)}[fmt]
    v = np.moveaxis(np.asarray(x, np.float32).astype(ml_dtypes.bfloat16).astype(np.float64), axis, -1)
    blocks = v.reshape(v.shape[:-1] + (-1, 32))
    amax = np.abs(blocks).max(-1, keepdims=True)
    byte = np.maximum(np.where(amax > 0, np.frexp(amax)[1] - 1 + 127, 0) - down, 1)
    scale = np.exp2(byte - 127.0)
    codes = (blocks / scale).astype(np.float32).astype(dtype).astype(np.float64)
    return np.moveaxis((codes * scale).reshape(v.shape), -1, axis)


WIDE = False


def mx_kscale(k):
    if not WIDE:
        return np.ones(k)
    levels = np.array([10, -10, 5, -5, 0])
    if k % 512:
        return np.exp2(np.random.permutation(np.resize(levels, k // 32))).repeat(32)
    a = np.empty((k // 512, 16))
    for p in range(k // 512):
        a[p, :8] = np.random.permutation(np.resize(levels, 8))
        for g in range(8):
            far = levels[np.abs(levels - a[p, g]) >= 10]
            a[p, g + 8] = far[np.random.randint(len(far))]
    return np.exp2(a.ravel()).repeat(32)


BF16 = ml_dtypes.bfloat16


def bf(x):
    return np.asarray(x, np.float32).astype(BF16)


def f64(x):
    return np.asarray(x).astype(np.float64)


E2M1 = np.array([0.0, 0.5, 1.0, 1.5, 2.0, 3.0, 4.0, 6.0, -0.0, -0.5, -1.0, -1.5, -2.0, -3.0, -4.0, -6.0])


def pack_weight(w, fmt):
    k, n = w.shape
    w = f64(bf(w)).reshape(k // 32, 32, n)
    amax = np.abs(w).max(1)
    if fmt == "e4m3":
        byte = np.frexp(amax)[1] - 1 + 127 - 7
    else:
        mant, ex = np.frexp(amax / 6.0)
        byte = np.where(mant > 0.5, ex, ex - 1) + 127
    byte = np.clip(np.where(amax > 0, byte, 1), 1, 254)
    scaled = (w * np.exp2(127.0 - byte)[:, None, :]).reshape(k, n).astype(np.float32)
    by_word = np.ascontiguousarray(scaled.reshape(k // 512, 128, 4, n).transpose(0, 1, 3, 2))
    if fmt == "e4m3":
        words = by_word.astype(ml_dtypes.float8_e4m3fn).view(np.uint8)
    else:
        c = by_word.astype(ml_dtypes.float4_e2m1fn).view(np.uint8) & 0xF
        words = c[..., 0::2] | (c[..., 1::2] << 4)
    return np.ascontiguousarray(words), np.ascontiguousarray(byte.astype(np.uint8).reshape(k // 512, 16, n))


def unpack_weight(words, scales, fmt):
    g, p, n, _ = words.shape
    if fmt == "e4m3":
        vals = np.ascontiguousarray(words).view(ml_dtypes.float8_e4m3fn).astype(np.float64)
    else:
        nib = np.empty((g, p, n, 4), np.uint8)
        nib[..., 0::2] = words & 0xF
        nib[..., 1::2] = words >> 4
        vals = E2M1[nib]
    vals = vals * np.repeat(np.exp2(scales.astype(np.float64) - 127.0), 8, axis=1)[..., None]
    return vals.transpose(0, 1, 3, 2).reshape(g * 512, n)
def pack4(w):
    words, scales = pack_weight(w, "e2m1")
    return words.reshape(words.shape[0], 128, -1), scales


def unpack4(words, scales):
    return unpack_weight(words.reshape(words.shape[0], 128, -1, 2), scales, "e2m1")


def planes(Y):
    n, m = Y.shape
    b = f64(bf(Y)).reshape(n // 32, 32, m)
    amax = np.abs(b).max(1)
    byte = np.clip(np.where(amax > 0, np.frexp(amax)[1] - 1 + 127 - 7, 1), 1, 254)
    codes = (b * np.exp2(127.0 - byte)[:, None, :]).reshape(n, m).astype(np.float32).astype(ml_dtypes.float8_e4m3fn).view(np.uint8)
    words = codes.reshape(n // 512, 128, 4, m).transpose(0, 1, 3, 2)
    return np.ascontiguousarray(words), np.ascontiguousarray(byte.astype(np.uint8).reshape(n // 512, 16, m))


B, P, R, KP, KR, N = 16, 8, 32, 2048, 4096, 1024


def setup_inputs():
    s = mx_kscale(KP)
    r = mx_kscale(KR)
    pep = bf(np.random.randn(B, P, KP) * s)
    rec = bf(np.random.randn(B, R, KR) * r)
    w_pep = bf(np.random.randn(KP, N) / np.sqrt(KP) / s[:, None])
    w_rec_words, w_rec_scales = pack4(np.random.randn(KR, N) / np.sqrt(KR) / r[:, None])
    pos = bf(0.5 * np.random.randn(P, R, N))
    gain = bf(np.exp(0.7 * np.random.randn(N)))
    return {"pep": pep, "rec": rec, "w_pep": w_pep, "w_rec_words": w_rec_words,
            "w_rec_scales": w_rec_scales, "pos": pos, "gain": gain}


def reference(pep, rec, w_pep, w_rec_words, w_rec_scales, pos, gain):
    a = mxq(f64(pep).reshape(B * P, KP), 1, "e4m3")
    wa = mxq(f64(w_pep), 0, "e4m3")
    left = (a @ wa).reshape(B, P, 1, N)
    c = mxq(f64(rec).reshape(B * R, KR), 1, "e4m3")
    wc = unpack4(w_rec_words, w_rec_scales)
    right = (c @ wc).reshape(B, 1, R, N)
    y = (left + right + f64(pos)) * f64(gain)
    Y = y.reshape(B * P * R, N).T
    words, scales = planes(Y)
    return y, words, scales

from contextlib import ExitStack

import concourse.mybir as mybir
from concourse.masks import make_identity

B, NI, NJ, KP, KR, N = 16, 8, 32, 2048, 4096, 1024
FLOPS = 2 * B * NI * KP * N + 2 * B * NJ * KR * N

F32 = mybir.dt.float32
BF16 = mybir.dt.bfloat16
U32 = mybir.dt.uint32
I32 = mybir.dt.int32
U8 = mybir.dt.uint8
FP8X4 = mybir.dt.float8_e4m3fn_x4
FP4X4 = mybir.dt.float4_e2m1fn_x4
MULT = mybir.AluOpType.mult
ADD = mybir.AluOpType.add
COPY = mybir.ActivationFunctionType.Copy
IDENTITY = mybir.ActivationFunctionType.Identity

P = 128
PACK = 4
GROUP = P * PACK
PEP_PASSES = KP // GROUP
REC_PASSES = KR // GROUP
PAIRS = NI * NJ
UNIT_B = 2
UNIT_M = UNIT_B * PAIRS
UNIT_LIST = [(g, b, UNIT_B) for g in range(2) for b in range(0, B, UNIT_B)][:-1] + [(1, B - 2, 1), (1, B - 1, 1)]
UNITS = len(UNIT_LIST)
Y_BUFS = 4
STAGE_BUFS = 5

SCALAR_BLOCKS = [2, 2, 2, 3, 2, 2, 2, 2, 2, 3, 3, 3, 3, 3, 2, 1, 2]
HEAD_ITEMS = 11
SLOT_ITEMS = [2, 3, 3, 3, 3, 3, 4, 4, 3, 3, 3, 3, 3, 3, 3, 3, 3]
W1_SLOTS = [1, 2, 2, 3, 3, 4, 4, 4]
LEAD = 3
V_ROWS = [(16, 0), (16, 1)]


def tile_peptide_pocket_pair_tensor_g5_kernel(
    tc, pep, rec, w_pep, w_rec_words, w_rec_scales, pos, gain, out_0, out_1, out_2
):
    nc = tc.nc
    with ExitStack() as ctx:
        sb = ctx.enter_context(tc.tile_pool(name="sb", bufs=1))
        ps = ctx.enter_context(tc.psum_pool(name="ps", bufs=1))
        ctx.enter_context(tc.manual_schedule(engines={mybir.EngineType.DVE, mybir.EngineType.Pool, mybir.EngineType.SP}))

        def sbuf(name, shape, dtype):
            return sb.tile(shape, dtype, name=name, align_bytes=64)

        def ring(name, count, shape, dtype):
            return [sbuf("%s%d" % (name, n), shape, dtype) for n in range(count)]

        bank = [ps.tile([P, GROUP], F32, name="bank%d" % n) for n in range(8)]
        pos_bank = [bank[0], bank[7]]
        right_bank = [bank[1], bank[2]]
        mx_bank = bank[3]
        turn_banks = [bank[4], bank[5], bank[6]]
        rec_bank = bank[7]
        turn_count = [0]

        def next_turn_bank():
            turn_count[0] += 1
            return turn_banks[turn_count[0] % len(turn_banks)]

        ident32 = sbuf("ident32", [P, P], F32)
        ident16 = sbuf("ident16", [P, P], BF16)
        gain16 = sbuf("gain16", [P, 2, PACK], BF16)
        gain32 = sbuf("gain32", [P, 2 * PACK], F32)
        pep_raw = sbuf("pep_raw", [P, KP], BF16)
        pos_raw = ring("pos_raw", 2, [P, 2, GROUP], BF16)
        pos_sb = ring("pos_sb", 2, [P, PACK, PAIRS], BF16)
        w_raw = ring("w_raw", PEP_PASSES, [P, PACK, GROUP], BF16)
        rec_raw = ring("rec_raw", 3, [P, KR], BF16)
        wr_words = ring("wr_words", 2, [P, REC_PASSES, 2 * GROUP], U8)
        wr_scales = ring("wr_scales", 2, [P, REC_PASSES, GROUP], U8)
        stage = ring("stage", STAGE_BUFS, [P, PACK * GROUP], BF16)
        pep_codes = sbuf("pep_codes", [P, PEP_PASSES * P], U32)
        pep_scales = sbuf("pep_scales", [P, PEP_PASSES * P], U8)
        w_codes = ring("w_codes", PEP_PASSES, [P, GROUP], U32)
        w_scales = ring("w_scales", PEP_PASSES, [P, GROUP], U8)
        rec_codes = ring("rec_codes", 8, [P, GROUP], U32)
        rec_scales = ring("rec_scales", 8, [P, GROUP], U8)
        right_sb = sbuf("right_sb", [P, PACK, P], F32)
        left_g = ring("left_g", 2, [P, PACK, P], F32)
        y32 = ring("y32", Y_BUFS, [P, PACK, UNIT_M], F32)
        y_rows = ring("y_rows", 3, [P, UNIT_M // P, GROUP], F32)
        y16 = sbuf("y16", [P, UNIT_M, PACK], BF16)
        y16_last = sbuf("y16_last", [P, PAIRS, PACK], BF16)
        y_codes = ring("y_codes", 3, [P, UNIT_M], U32)
        y_scales = ring("y_scales", 2, [P, B * PAIRS], U8)
        free_stages = list(range(STAGE_BUFS))

        def next_stage():
            assert len(free_stages) > 0
            first = free_stages[0]
            free_stages.remove(first)
            return first

        rec_rows = rec.rearrange("b j f -> (b j) f")
        out_rows = out_0.rearrange("b i j c -> (b i j) c")

        def cols(g):
            return slice(GROUP * g, GROUP * (g + 1))

        def gain_col(g, t):
            return gain32[:, PACK * g + t : PACK * g + t + 1]

        def load_w(g, k):
            rows = w_pep[GROUP * k : GROUP * (k + 1), cols(g)]
            nc.sync.dma_start(out=w_raw[k][:], in_=rows.rearrange("(p j) c -> p j c", j=PACK))

        def load_pos(g):
            view = pos.rearrange("(h i) j c -> (i j) h c", h=2)
            nc.sync.dma_start(out=pos_raw[g][:], in_=view[:, :, cols(g)])

        def load_rec(q, parts):
            width = KR // parts
            for n in range(parts):
                f = slice(width * n, width * (n + 1))
                nc.sync.dma_start(out=rec_raw[q % 3][:, f], in_=rec_rows[P * q : P * (q + 1), f])

        def load_wr(g, parts):
            for quad in range(4):
                rows = w_rec_scales[:, 4 * quad : 4 * quad + 4, cols(g)].rearrange("k r n -> r k n")
                nc.sync.dma_start(
                    out=wr_scales[g][32 * quad : 32 * quad + 4, :, :].bitcast(I32), in_=rows.bitcast(I32)
                )
            words = w_rec_words[:, :, 2 * GROUP * g : 2 * GROUP * (g + 1)].rearrange("k p n -> p k n")
            step = REC_PASSES // parts
            for k in range(0, REC_PASSES, step):
                nc.sync.dma_start(
                    out=wr_words[g][:, k : k + step, :].bitcast(I32), in_=words[:, k : k + step, :].bitcast(I32)
                )

        def quantize(codes, scales, grouped):
            nc.vector.quantize_mx(out=codes.bitcast(FP8X4), scales=scales, in_=grouped)

        def quantize_stage(codes, scales, grouped):
            quantize(codes[:], scales[:], stage[grouped][:])
            free_stages.append(grouped)

        def turn_tokens(raw, k0, psum):
            words = raw[:].bitcast(F32)
            view = psum[:].rearrange("p (k u r) -> p k u r", k=2, u=2)
            for kk in range(2):
                for u in range(2):
                    first = 256 * (k0 + kk)
                    nc.tensor.transpose(view[:, kk, u, :], words[:, first + u : first + 256 : 2], ident32[:])

        def group_tokens(psum, grouped, part):
            words = stage[grouped][:].bitcast(F32)[:, GROUP * part : GROUP * (part + 1)]
            nc.scalar.copy(
                out=words.rearrange("p (k r u) -> p k r u", k=2, u=2),
                in_=psum[:].rearrange("p (k u r) -> p k r u", k=2, u=2),
            )

        def interleave_w(engine, k, grouped, half):
            src = w_raw[k][:].rearrange("p j (m t) -> p t m j", t=PACK)[:, 2 * half : 2 * half + 2]
            dst = stage[grouped][:].rearrange("p (t m j) -> p t m j", t=PACK, j=PACK)[:, 2 * half : 2 * half + 2]
            if engine == "v":
                nc.vector.tensor_copy(out=dst, in_=src)
            elif engine == "s":
                nc.scalar.copy(out=dst, in_=src)
            else:
                nc.gpsimd.tensor_scalar(out=dst, in0=src, scalar1=1.0, scalar2=0.0, op0=MULT, op1=ADD)

        def left_pass(out, t, k):
            nc.tensor.matmul_mx(
                out=out,
                lhsT=w_codes[k][:, P * t : P * (t + 1)].bitcast(FP8X4),
                lhsT_scale=w_scales[k][:, P * t : P * (t + 1)],
                rhs=pep_codes[:, P * k : P * (k + 1)].bitcast(FP8X4),
                rhs_scale=pep_scales[:, P * k : P * (k + 1)],
                start=(k == 0),
                stop=(k == PEP_PASSES - 1),
            )

        def left_out(g, t, psum):
            nc.scalar.activation(out=left_g[g][:, t, :], in_=psum, func=COPY, scale=gain_col(g, t))

        def pos_view(g):
            return pos_bank[g][:].bitcast(BF16).rearrange("p (t m) -> p t m", t=PACK)

        def turn_pos(g):
            for t in range(PACK):
                for h in range(2):
                    nc.tensor.transpose(
                        pos_view(g)[:, t, P * h : P * (h + 1)], pos_raw[g][:, h, t:GROUP:PACK], ident16[:]
                    )
            nc.scalar.copy(out=pos_sb[g][:], in_=pos_view(g))

        def right_passes(job, k0, k1):
            g, q = divmod(job, 4)
            for k in range(k0, k1):
                half, kk = divmod(k, 4)
                nc.tensor.matmul_mx(
                    out=mx_bank[:],
                    lhsT=rec_codes[2 * q + half][:, P * kk : P * (kk + 1)].bitcast(FP8X4),
                    lhsT_scale=rec_scales[2 * q + half][:, P * kk : P * (kk + 1)],
                    rhs=wr_words[g][:, k, :].bitcast(FP4X4),
                    rhs_scale=wr_scales[g][:, k, :],
                    start=(k == 0),
                    stop=(k == REC_PASSES - 1),
                )

        def right_out():
            nc.scalar.copy(out=right_sb[:], in_=mx_bank[:].rearrange("r (p t) -> r t p", t=PACK))

        def right_turn(job):
            for t in range(PACK):
                nc.tensor.transpose(right_bank[job % 2][:, P * t : P * (t + 1)], right_sb[:, t, :], ident32[:])

        def first_sum_vector(unit, t, b0, nb):
            g, first_b, size = UNIT_LIST[unit]
            shape = [P, nb, NI, NJ]
            first = NI * (first_b + b0)
            out = y32[unit % Y_BUFS][:, t, PAIRS * b0 : PAIRS * (b0 + nb)]
            nc.vector.scalar_tensor_tensor(
                out=out.rearrange("p (b i j) -> p b i j", i=NI, j=NJ),
                in0=pos_view(g)[:, t, :].rearrange("p (i j) -> p i j", j=NJ).unsqueeze(1).to_broadcast(shape),
                scalar=gain_col(g, t),
                in1=left_g[g][:, t, first : first + NI * nb]
                .rearrange("p (b i) -> p b i", i=NI)
                .unsqueeze(3)
                .to_broadcast(shape),
                op0=MULT,
                op1=ADD,
            )

        def first_sum_scalar(unit, t, b):
            g, first_b, size = UNIT_LIST[unit]
            for i in range(NI):
                token = NI * (first_b + b) + i
                m0 = PAIRS * b + NJ * i
                nc.scalar.activation(
                    out=y32[unit % Y_BUFS][:, t, m0 : m0 + NJ],
                    in_=pos_sb[g][:, t, NJ * i : NJ * (i + 1)],
                    func=IDENTITY,
                    bias=left_g[g][:, t, token : token + 1],
                    scale=gain_col(g, t),
                )

        def second_sum(unit, n0=0, n1=8):
            g, first_b, size = UNIT_LIST[unit]
            for n in range(n0, min(n1, PACK * size)):
                    b, t = divmod(n, PACK)
                    token = P * t + NJ * ((first_b + b) % 4)
                    y = y32[unit % Y_BUFS][:, t, PAIRS * b : PAIRS * (b + 1)].rearrange("p (i j) -> p i j", j=NJ)
                    right = right_bank[((first_b + b) // 4) % 2][:, token : token + NJ]
                    nc.vector.scalar_tensor_tensor(
                        out=y,
                        in0=right.unsqueeze(1).to_broadcast([P, NI, NJ]),
                        scalar=gain_col(g, t),
                        in1=y,
                        op0=MULT,
                        op1=ADD,
                    )

        def rows(unit, mt):
            psum = next_turn_bank()
            for t in range(PACK):
                nc.tensor.transpose(
                    psum[:, P * t : P * (t + 1)], y32[unit % Y_BUFS][:, t, P * mt : P * (mt + 1)], ident32[:]
                )
            dst = y_rows[unit % 3][:, mt, :].rearrange("m (p t) -> m p t", t=PACK)
            src = psum[:].rearrange("m (t p) -> m p t", t=PACK)
            if (unit, mt) in V_ROWS:
                nc.vector.tensor_copy(out=dst, in_=src)
            else:
                nc.scalar.copy(out=dst, in_=src)

        def store_rows(unit):
            g, first_b, size = UNIT_LIST[unit]
            dst = out_rows[PAIRS * first_b : PAIRS * (first_b + size), cols(g)]
            nc.sync.dma_start(out=dst.rearrange("(mt m) c -> m mt c", m=P), in_=y_rows[unit % 3][:, 0 : 2 * size, :])

        def round_unit(unit):
            width = PAIRS * UNIT_LIST[unit][2]
            src = y32[unit % Y_BUFS][:, :, 0:width].rearrange("p t m -> p m t")
            if unit == UNITS - 1:
                nc.scalar.copy(out=y16_last[:], in_=src)
            else:
                nc.gpsimd.tensor_scalar(out=y16[:, 0:width, :], in0=src, scalar1=1.0, scalar2=0.0, op0=MULT, op1=ADD)

        def quantize_unit(unit):
            g, first_b, size = UNIT_LIST[unit]
            width = PAIRS * size
            m_cols = slice(PAIRS * first_b, PAIRS * first_b + width)
            codes = y_codes[unit % 3][:, 0:width]
            rounded = y16_last if unit == UNITS - 1 else y16
            quantize(codes, y_scales[g][:, m_cols], rounded[:, 0:width, :].rearrange("p m t -> p (m t)"))
            words = out_1[g].rearrange("p m t -> p (m t)").bitcast(I32)
            nc.sync.dma_start(out=words[:, m_cols], in_=codes.bitcast(I32))

        def store_scales(g, m0, m1):
            for quad in range(4):
                nc.sync.dma_start(
                    out=out_2[g, 4 * quad : 4 * quad + 4, m0:m1].bitcast(I32),
                    in_=y_scales[g][32 * quad : 32 * quad + 4, m0:m1].bitcast(I32),
                )

        scalar_blocks = []
        items = []
        for unit in range(UNITS):
            size = UNIT_LIST[unit][2]
            blocks = [(t, b) for t in range(PACK) for b in range(size)]
            scalar_blocks.append(blocks[len(blocks) - SCALAR_BLOCKS[unit] :])
            for t in range(PACK):
                mine = [b for b in range(size) if (t, b) not in scalar_blocks[unit]]
                if mine:
                    items.append((unit, t, mine[0], len(mine)))
        done = [0]

        def first_sums(count, up_to_unit, must_unit):
            while done[0] < len(items) and items[done[0]][0] <= up_to_unit:
                if count <= 0 and items[done[0]][0] > must_unit:
                    break
                first_sum_vector(*items[done[0]])
                done[0] += 1
                count -= 1

        def scalar_sums(unit):
            for t, b in scalar_blocks[unit]:
                first_sum_scalar(unit, t, b)

        nc.sync.dma_start(out=pep_raw[:], in_=pep.rearrange("b i e -> (b i) e"))
        nc.sync.dma_start(out=gain16[:], in_=gain.rearrange("(g p t) -> p g t", g=2, t=PACK))
        for k in range(PEP_PASSES):
            load_w(0, k)
            if k == 1:
                load_pos(0)
        load_rec(0, 2)
        make_identity(nc, ident32[:])
        make_identity(nc, ident16[:])
        for g in range(2):
            nc.vector.memset(wr_scales[g][:].rearrange("p k n -> p (k n)").bitcast(I32), 0)
        load_wr(0, 2)
        load_rec(1, 1)
        load_rec(2, 1)
        nc.scalar.activation(out=gain32[:], in_=gain16[:].rearrange("p g t -> p (g t)"), func=COPY)

        pep_grouped = next_stage()
        for part in range(2):
            psum = next_turn_bank()
            turn_tokens(pep_raw, 2 * part, psum)
            group_tokens(psum, pep_grouped, part)
        left_banks = [bank[1], bank[2], bank[3], bank[7]]
        w_grouped = []
        for k in range(PEP_PASSES + 1):
            if k < PEP_PASSES:
                w_grouped.append(next_stage())
                interleave_w("v", k, w_grouped[k], 0)
                interleave_w("s", k, w_grouped[k], 1)
            if k == 0:
                quantize_stage(pep_codes, pep_scales, pep_grouped)
            else:
                quantize_stage(w_codes[k - 1], w_scales[k - 1], w_grouped[k - 1])
                if k == PEP_PASSES - 1:
                    turn_pos(0)
                for t in range(PACK):
                    left_pass(left_banks[t][:, 0:P], t, k - 1)
        for t in range(PACK):
            left_out(0, t, left_banks[t][:, 0:P])

        rec_grouped = {}

        def rec_part(q, half, part, psum):
            if part == 0:
                rec_grouped[(q, half)] = next_stage()
            turn_tokens(rec_raw[q % 3], 4 * half + 2 * part, psum)
            group_tokens(psum, rec_grouped[(q, half)], part)

        def quantize_rec(q, half):
            quantize_stage(rec_codes[2 * q + half], rec_scales[2 * q + half], rec_grouped[(q, half)])

        for half in range(2):
            for part in range(2):
                rec_part(0, half, part, next_turn_bank())
        load_rec(3, 1)
        for k in range(PEP_PASSES):
            load_w(1, k)
        load_pos(1)
        load_wr(1, 1)
        first_sums(2, 3, -1)
        quantize_rec(0, 0)
        first_sums(1, 3, -1)
        quantize_rec(0, 1)
        scalar_sums(0)
        right_passes(0, 0, 4)
        rec_part(1, 0, 0, next_turn_bank())
        right_passes(0, 4, 8)
        scalar_sums(1)
        rec_part(1, 0, 1, next_turn_bank())
        right_out()
        right_turn(0)
        rec_part(1, 1, 0, next_turn_bank())
        rec_part(1, 1, 1, next_turn_bank())
        first_sums(HEAD_ITEMS - 3, 3, 0)
        second_sum(0, 0, 4)
        quantize_rec(1, 0)
        second_sum(0, 4, 7)
        quantize_rec(1, 1)
        second_sum(0, 7, 8)
        round_unit(0)

        w1_grouped = {}
        for s in range(UNITS - 1):
            size = UNIT_LIST[s][2]
            job = s // 2 + 1
            if s < 4:
                rec_part(2 + s // 2, s % 2, 0, rec_bank)
            if s + 2 < UNITS and s != 6:
                scalar_sums(s + 2)
            if s == 7:
                scalar_sums(8)
            rows(s, 0)
            if s < 4:
                rec_part(2 + s // 2, s % 2, 1, rec_bank)
            rows(s, 1)
            if s == 0:
                right_passes(1, 0, 8)
            elif s % 2 == 0 and job < 8:
                right_passes(job, 6, 8)
            elif s % 2 == 1 and job + 1 < 8:
                right_passes(job + 1, 2, 4)
            if size == 2:
                rows(s, 2)
            if s % 2 == 0 and job < 8:
                right_out()
            if size == 2:
                rows(s, 3)
            if s % 2 == 0 and job < 8:
                right_turn(job)
            store_rows(s)
            for n in range(len(W1_SLOTS)):
                if W1_SLOTS[n] == s:
                    k, half = divmod(n, 2)
                    if half == 0:
                        w1_grouped[k] = next_stage()
                    interleave_w("s", k, w1_grouped[k], half)
            if s == 5:
                turn_pos(1)

            first_sums(SLOT_ITEMS[s], min(s + LEAD, 7) if s < 7 else s + LEAD, s + 1)
            second_sum(s + 1)
            if s == UNITS - 2:
                round_unit(s + 1)
                rows(s + 1, 0)
                rows(s + 1, 1)
                store_rows(s + 1)
            for k in range(PEP_PASSES):
                if W1_SLOTS[2 * k + 1] + 1 == s:
                    quantize_stage(w_codes[k], w_scales[k], w1_grouped[k])
            if s < 4:
                quantize_rec(2 + s // 2, s % 2)
            quantize_unit(s)
            if s == 7:
                store_scales(0, 0, B * PAIRS)
            if s == UNITS - 4:
                store_scales(1, 0, B * PAIRS - 4 * PAIRS)
            if s == UNITS - 2:
                quantize_unit(s + 1)
                store_scales(1, B * PAIRS - 4 * PAIRS, B * PAIRS)
            else:
                round_unit(s + 1)

            if s % 2 == 0 and job + 1 < 8:
                right_passes(job + 1, 0, 2)
            elif s % 2 == 1 and job + 1 < 8:
                right_passes(job + 1, 4, 6)
            if s == W1_SLOTS[-1] + 1:
                psum = next_turn_bank()
                for t in range(PACK):
                    for k in range(PEP_PASSES):
                        left_pass(psum[:, P * t : P * (t + 1)], t, k)
                for t in range(PACK):
                    left_out(1, t, psum[:, P * t : P * (t + 1)])
